import numpy as np
import ml_dtypes


def mxq(x, axis, fmt="e4m3"):
    dtype, down = {"e4m3": (ml_dtypes.float8_e4m3fn, 7), "e5m2": (ml_dtypes.float8_e5m2, 14)}[fmt]
    v = np.moveaxis(np.asarray(x, np.float32).astype(ml_dtypes.bfloat16).astype(np.float64), axis, -1)
    blocks = v.reshape(v.shape[:-1] + (-1, 32))
    amax = np.abs(blocks).max(-1, keepdims=True)
    byte = np.maximum(np.where(amax > 0, np.frexp(amax)[1] - 1 + 127, 0) - down, 1)
    scale = np.exp2(byte - 127.0)
    codes = (blocks / scale).astype(np.float32).astype(dtype).astype(np.float64)
    return np.moveaxis((codes * scale).reshape(v.shape), -1, axis)


WIDE = False


def mx_kscale(k):
    if not WIDE:
        return np.ones(k)
    levels = np.array([10, -10, 5, -5, 0])
    if k % 512:
        return np.exp2(np.random.permutation(np.resize(levels, k // 32))).repeat(32)
    a = np.empty((k // 512, 16))
    for p in range(k // 512):
        a[p, :8] = np.random.permutation(np.resize(levels, 8))
        for g in range(8):
            far = levels[np.abs(levels - a[p, g]) >= 10]
            a[p, g + 8] = far[np.random.randint(len(far))]
    return np.exp2(a.ravel()).repeat(32)


BF16 = ml_dtypes.bfloat16


def bf(x):
    return np.asarray(x, np.float32).astype(BF16)


def f64(x):
    return np.asarray(x).astype(np.float64)


B, N, D = 1, 1024, 512


def channel_logits(q, k, tau):
    n_tokens = q.shape[1]
    s = mxq(q, 1, "e4m3").transpose(0, 2, 1) @ mxq(k, 1, "e4m3")
    return s * tau[None, :, None] / np.sqrt(n_tokens)


def softmax(l):
    e = np.exp(l - l.max(-1, keepdims=True))
    return e / e.sum(-1, keepdims=True)


def draw0():
    s, t = mx_kscale(N), mx_kscale(D)
    return {"q": bf(np.random.standard_normal((B, N, D)) * s[None, :, None]),
            "k": bf(np.random.standard_normal((B, N, D)) / s[None, :, None]),
            "v": bf(np.random.standard_normal((B, N, D)) / t[None, None, :]),
            "tau": bf(np.random.uniform(1.5, 2.5, D)),
            "gain": bf((1.0 + 0.1 * np.random.standard_normal(D)) * t)}


def core(q, k, v, tau, gain):
    q, k, v, tau, gain = f64(q), f64(k), f64(v), f64(tau), f64(gain)
    d = q.shape[-1]
    l = channel_logits(q, k, tau)
    a = softmax(l)
    c = (a - 1.0 / d) * gain[None, None, :]
    return mxq(v, 2, "e4m3") @ mxq(c, 2, "e4m3").transpose(0, 2, 1)


def e4m3fn_bytes(y):
    return np.clip(np.asarray(y, np.float64), -448.0, 448.0).astype(np.float32).astype(ml_dtypes.float8_e4m3fn).view(np.uint8)


def e4m3fn_values(b):
    return np.asarray(b, np.uint8).view(ml_dtypes.float8_e4m3fn).astype(np.float64)


def setup_inputs():
    d = draw0()
    x0 = np.asarray(d['v']).astype(np.float64)
    s = (np.max(np.abs(x0), axis=(0, 1), keepdims=True) / 448.0).astype(np.float32)
    out = {}
    for k, v in d.items():
        if k == 'v':
            out['v_bytes'] = e4m3fn_bytes(x0 / s.astype(np.float64))
            out['v_scale'] = s
        else:
            out[k] = v
    return out


def reference(q, k, v_bytes, v_scale, tau, gain):
    return core(q, k, e4m3fn_values(v_bytes) * v_scale.astype(np.float64), tau, gain)

@@ -1,0 +1,305 @@
+from contextlib import ExitStack
+
+import concourse.mybir as mybir
+from concourse.masks import make_identity
+
+N, D = 1024, 512
+FLOPS = 2 * 2 * N * D * D
+
+F32 = mybir.dt.float32
+BF16 = mybir.dt.bfloat16
+U32 = mybir.dt.uint32
+U8 = mybir.dt.uint8
+FP8 = mybir.dt.float8_e4m3fn
+FP8X4 = mybir.dt.float8_e4m3fn_x4
+ALU = mybir.AluOpType
+ACT = mybir.ActivationFunctionType
+
+P = 128
+PACK = 4
+PASSES = N // (P * PACK)
+TILES = D // P
+V_HALVES = 2
+V_ROWS = N // (V_HALVES * P)
+V_PAIRS = N // (2 * P)
+K1_SCALAR_COLS = 320
+
+
+def tile_scaledchannelattentioncentredmap_kernel(tc, q, k, v_bytes, v_scale, tau, gain, out):
+    nc = tc.nc
+    with ExitStack() as ctx:
+        keep = ctx.enter_context(tc.tile_pool(name="keep", bufs=1))
+        work = ctx.enter_context(tc.tile_pool(name="work", bufs=4))
+        psum = ctx.enter_context(tc.psum_pool(name="psum", bufs=2))
+        ctx.enter_context(tc.manual_schedule())
+
+        ident = keep.tile([P, P], F32, name="ident")
+        ident_bf = keep.tile([P, P], BF16, name="ident_bf")
+        tau_rows = keep.tile([P, P], BF16, name="tau_rows")
+        neg_tau = keep.tile([P, TILES], F32, name="neg_tau")
+        gain_col = keep.tile([P, PACK], BF16, name="gain_col")
+        scale_col = keep.tile([P, PACK], F32, name="scale_col")
+        v_raw = [keep.tile([P, V_ROWS, D], U8, name="v_raw%d" % h, align_bytes=256) for h in range(V_HALVES)]
+        k_raw = [keep.tile([P, PACK, D], BF16, name="k_raw%d" % g, align_bytes=256) for g in range(PASSES)]
+        q_raw = keep.tile([P, PASSES, PACK, D], BF16, name="q_raw", align_bytes=256)
+        k_grouped = [keep.tile([P, D, PACK], BF16, name="k_grouped%d" % g, align_bytes=64) for g in range(PASSES)]
+        k_codes = [keep.tile([P, D], U32, name="k_codes%d" % g, align_bytes=64) for g in range(PASSES)]
+        k_scales = [keep.tile([P, D], U8, name="k_scales%d" % g, align_bytes=64) for g in range(PASSES)]
+        v_codes = [keep.tile([P, 2 * P], U32, name="v_codes%d" % b, align_bytes=64) for b in range(V_PAIRS)]
+        v_scales = [keep.tile([P, 2 * P], U8, name="v_scales%d" % b, align_bytes=64) for b in range(V_PAIRS)]
+
+        nc.gpsimd.memset(tau_rows[:], 0.0)
+        make_identity(nc, ident[:])
+        nc.scalar.dma_start(out=scale_col[:], in_=v_scale.rearrange("a b (p t) -> p (a b t)", t=PACK))
+        nc.scalar.dma_start(out=gain_col[:], in_=gain.rearrange("(p t) -> p t", t=PACK))
+        nc.scalar.dma_start(out=tau_rows[0:TILES, :], in_=tau.rearrange("(a p) -> a p", p=P))
+        v_rows = v_bytes[0].rearrange("(h p r) j -> h p r j", p=P, r=V_ROWS)
+        k_rows = k[0].rearrange("(g p t) c -> g p t c", p=P, t=PACK)
+        q_rows = q[0].rearrange("(g p t) c -> g p t c", p=P, t=PACK)
+        out_rows = out[0].rearrange("(h p r) i -> h p r i", p=P, r=V_ROWS)
+        nc.sync.dma_start(out=v_raw[0][:], in_=v_rows[0])
+        nc.sync.dma_start(out=k_raw[0][:], in_=k_rows[0])
+        nc.sync.dma_start(out=v_raw[1][:], in_=v_rows[1])
+        nc.sync.dma_start(out=k_raw[1][:], in_=k_rows[1])
+        for g in range(PASSES):
+            nc.sync.dma_start(out=q_raw[:, g], in_=q_rows[g])
+        nc.scalar.activation(out=ident_bf[:], in_=ident[:], func=ACT.Copy)
+
+        scale_bank = psum.tile([P, P, PACK], F32, name="scale_bank", tag="o", bufs=4)
+        for t in range(PACK):
+            nc.tensor.transpose(scale_bank[:, :, t], scale_col[:, t : t + 1].to_broadcast([P, P]), ident[:])
+        tau_bank = psum.tile([P, P], BF16, name="tau_bank", tag="o", bufs=4)
+        nc.tensor.transpose(tau_bank[:], tau_rows[:], ident_bf[:])
+
+        def interleave(engine, dst, src):
+            if engine is nc.scalar:
+                engine.copy(out=dst, in_=src)
+            else:
+                engine.tensor_copy(out=dst, in_=src)
+
+        def k_interleave(engine, g, c0, c1):
+            interleave(
+                engine,
+                k_grouped[g][:, c0:c1, :].rearrange("p (c i) t -> p c t i", i=4),
+                k_raw[g][:, :, c0:c1].rearrange("p t (c i) -> p c t i", i=4),
+            )
+
+        def k_quantize(g):
+            nc.vector.quantize_mx(
+                out=k_codes[g][:].bitcast(FP8X4), scales=k_scales[g][:], in_=k_grouped[g][:].rearrange("p c t -> p (c t)")
+            )
+
+        v_bf, v_bank, v_grouped = {}, {}, {}
+
+        def v_widen(b):
+            h, r0 = divmod(2 * b, V_ROWS)
+            v_bf[b] = work.tile([P, 2, D], BF16, name="v_bf", align_bytes=64)
+            for r in range(2):
+                nc.vector.tensor_tensor(
+                    out=v_bf[b][:, r, :],
+                    in0=v_raw[h][:, r0 + r, :].bitcast(FP8),
+                    in1=scale_bank[:].rearrange("p m t -> p (m t)"),
+                    op=ALU.mult,
+                )
+
+        def v_turn(b):
+            v_bank[b] = psum.tile([P, 2, 2, P], F32, name="v_bank", tag="tr")
+            for r in range(2):
+                words = v_bf[b][:, r, :].bitcast(F32)
+                for u in range(2):
+                    nc.tensor.transpose(v_bank[b][:, r, u, :], words[:, u : 2 * P : 2], ident[:])
+
+        def v_copy_out(b):
+            v_grouped[b] = work.tile([P, 2, P, 2], F32, name="v_grouped", align_bytes=64)
+            nc.scalar.copy(out=v_grouped[b][:], in_=v_bank[b][:].rearrange("p r u n -> p r n u"))
+
+        def v_quantize(b):
+            nc.vector.quantize_mx(
+                out=v_codes[b][:].bitcast(FP8X4),
+                scales=v_scales[b][:],
+                in_=v_grouped[b][:].rearrange("p r n u -> p (r n u)").bitcast(BF16),
+            )
+
+        q_grouped, q_codes, q_scales, s_bank, neg_l, neg_max, e, row_sum = {}, {}, {}, {}, {}, {}, {}, {}
+        a_map, a_bank, c_grouped, c_codes, c_scales, o_bank = {}, {}, {}, {}, {}, {}
+
+        def q_interleave(engine, a):
+            q_grouped[a] = work.tile([P, PASSES, P, PACK], BF16, name="q_grouped", align_bytes=64)
+            interleave(
+                engine,
+                q_grouped[a][:].rearrange("p g (c i) t -> p g c t i", i=4),
+                q_raw[:, :, :, P * a : P * (a + 1)].rearrange("p g t (c i) -> p g c t i", i=4),
+            )
+
+        def q_quantize(a):
+            q_codes[a] = work.tile([P, PASSES * P], U32, name="q_codes", align_bytes=64)
+            q_scales[a] = work.tile([P, PASSES * P], U8, name="q_scales", align_bytes=64)
+            nc.vector.quantize_mx(
+                out=q_codes[a][:].bitcast(FP8X4), scales=q_scales[a][:], in_=q_grouped[a][:].rearrange("p g c t -> p (g c t)")
+            )
+
+        def logits(a):
+            s_bank[a] = psum.tile([P, D], F32, name="s_bank", tag="s")
+            for g in range(PASSES):
+                nc.tensor.matmul_mx(
+                    out=s_bank[a][:],
+                    lhsT=q_codes[a][:, P * g : P * (g + 1)].bitcast(FP8X4),
+                    lhsT_scale=q_scales[a][:, P * g : P * (g + 1)],
+                    rhs=k_codes[g][:].bitcast(FP8X4),
+                    rhs_scale=k_scales[g][:],
+                    start=(g == 0),
+                    stop=(g == PASSES - 1),
+                )
+
+        def row_max(a):
+            neg_l[a] = work.tile([P, PACK, P], F32, name="neg_l")
+            neg_max[a] = work.tile([P, 1], F32, name="neg_max")
+            nc.vector.tensor_scalar(
+                out=neg_l[a][:],
+                in0=s_bank[a][:].rearrange("p (m t) -> p t m", t=PACK),
+                scalar1=neg_tau[:, a : a + 1],
+                scalar2=None,
+                op0=ALU.mult,
+                op1=ALU.min,
+                accum_out=neg_max[a][:],
+            )
+
+        def exponentials(a):
+            e[a] = work.tile([P, D], F32, name="e")
+            row_sum[a] = work.tile([P, 1], F32, name="row_sum")
+            nc.scalar.activation(
+                out=e[a][:],
+                in_=neg_l[a][:].rearrange("p t m -> p (t m)"),
+                func=ACT.Exp,
+                scale=-1.0,
+                bias=neg_max[a][:],
+                accum_out=row_sum[a][:],
+            )
+
+        inv_sum = {}
+
+        def invert(a):
+            inv_sum[a] = work.tile([P, 1], F32, name="inv_sum")
+            nc.vector.reciprocal(out=inv_sum[a][:], in_=row_sum[a][:])
+
+        def normalise(a):
+            a_map[a] = work.tile([P, D], F32, name="a_map")
+            nc.vector.tensor_scalar(out=a_map[a][:], in0=e[a][:], scalar1=inv_sum[a][:], scalar2=None, op0=ALU.mult)
+
+        def map_turn(a):
+            a_bank[a] = psum.tile([P, PACK, P], F32, name="a_bank", tag="tr")
+            for t in range(PACK):
+                nc.tensor.transpose(a_bank[a][:, t, :], a_map[a][:, P * t : P * (t + 1)], ident[:])
+
+        def centre(a):
+            c_grouped[a] = work.tile([P, P, PACK], BF16, name="c_grouped", align_bytes=64)
+            nc.vector.scalar_tensor_tensor(
+                out=c_grouped[a][:],
+                in0=a_bank[a][:].rearrange("p t i -> p i t"),
+                scalar=1.0 / D,
+                in1=gain_col[:].unsqueeze(1).to_broadcast([P, P, PACK]),
+                op0=ALU.subtract,
+                op1=ALU.mult,
+            )
+
+        def c_quantize(a):
+            c_codes[a] = work.tile([P, P], U32, name="c_codes", align_bytes=64)
+            c_scales[a] = work.tile([P, P], U8, name="c_scales", align_bytes=64)
+            nc.vector.quantize_mx(
+                out=c_codes[a][:].bitcast(FP8X4), scales=c_scales[a][:], in_=c_grouped[a][:].rearrange("p i t -> p (i t)")
+            )
+
+        def mix(a):
+            for h in range(V_HALVES):
+                o_bank[a, h] = psum.tile([P, V_ROWS, P], F32, name="o_bank", tag="o", bufs=4)
+                for r in range(V_ROWS):
+                    b, s = divmod(h * V_ROWS + r, 2)
+                    nc.tensor.matmul_mx(
+                        out=o_bank[a, h][:, r, :],
+                        lhsT=v_codes[b][:, P * s : P * (s + 1)].bitcast(FP8X4),
+                        lhsT_scale=v_scales[b][:, P * s : P * (s + 1)],
+                        rhs=c_codes[a][:].bitcast(FP8X4),
+                        rhs_scale=c_scales[a][:],
+                        start=True,
+                        stop=True,
+                    )
+
+        def store(engine, a, h):
+            result = work.tile([P, V_ROWS, P], F32, name="result", align_bytes=256, bufs=8)
+            interleave(engine, result[:], o_bank[a, h][:])
+            nc.sync.dma_start(out=out_rows[h][:, :, P * a : P * (a + 1)], in_=result[:])
+
+        v_widen(0)
+        v_turn(0)
+        k_interleave(nc.scalar, 0, 0, D)
+        v_widen(1)
+        v_turn(1)
+        v_widen(2)
+        v_widen(3)
+        nc.scalar.activation(out=neg_tau[:], in_=tau_bank[:, 0:TILES], func=ACT.Copy, scale=-1.0 / 32.0)
+        v_copy_out(0)
+        v_turn(2)
+        v_copy_out(1)
+        v_turn(3)
+        k_quantize(0)
+        k_interleave(nc.scalar, 1, 0, K1_SCALAR_COLS)
+        k_interleave(nc.vector, 1, K1_SCALAR_COLS, D)
+        q_interleave(nc.vector, 0)
+        v_quantize(0)
+        q_quantize(0)
+        k_quantize(1)
+        logits(0)
+        q_interleave(nc.scalar, 1)
+        v_quantize(1)
+        q_quantize(1)
+        logits(1)
+        row_max(0)
+        q_interleave(nc.scalar, 2)
+        exponentials(0)
+        q_quantize(2)
+        logits(2)
+        row_max(1)
+        v_copy_out(2)
+        v_copy_out(3)
+        exponentials(1)
+        q_interleave(nc.scalar, 3)
+        invert(0)
+        v_quantize(2)
+        normalise(0)
+        map_turn(0)
+        v_quantize(3)
+        invert(1)
+        row_max(2)
+        exponentials(2)
+        q_quantize(3)
+        logits(3)
+        normalise(1)
+        map_turn(1)
+        centre(0)
+        invert(2)
+        c_quantize(0)
+        mix(0)
+        row_max(3)
+        exponentials(3)
+        normalise(2)
+        map_turn(2)
+        centre(1)
+        invert(3)
+        c_quantize(1)
+        store(nc.scalar, 0, 0)
+        store(nc.scalar, 0, 1)
+        mix(1)
+        normalise(3)
+        map_turn(3)
+        centre(2)
+        store(nc.scalar, 1, 0)
+        store(nc.scalar, 1, 1)
+        c_quantize(2)
+        mix(2)
+        centre(3)
+        store(nc.scalar, 2, 0)
+        store(nc.scalar, 2, 1)
+        c_quantize(3)
+        mix(3)
+        store(nc.scalar, 3, 0)
+        store(nc.vector, 3, 1)

@@ -22,7 +22,6 @@ TILES = D // P
 V_HALVES = 2
 V_ROWS = N // (V_HALVES * P)
 V_PAIRS = N // (2 * P)
-K1_SCALAR_COLS = 320
 
 
 def tile_scaledchannelattentioncentredmap_kernel(tc, q, k, v_bytes, v_scale, tau, gain, out):
@@ -30,7 +29,7 @@ def tile_scaledchannelattentioncentredmap_kernel(tc, q, k, v_bytes, v_scale, tau
     with ExitStack() as ctx:
         keep = ctx.enter_context(tc.tile_pool(name="keep", bufs=1))
         work = ctx.enter_context(tc.tile_pool(name="work", bufs=4))
-        psum = ctx.enter_context(tc.psum_pool(name="psum", bufs=2))
+        psum = ctx.enter_context(tc.psum_pool(name="psum", bufs=1))
         ctx.enter_context(tc.manual_schedule())
 
         ident = keep.tile([P, P], F32, name="ident")
@@ -39,46 +38,45 @@ def tile_scaledchannelattentioncentredmap_kernel(tc, q, k, v_bytes, v_scale, tau
         neg_tau = keep.tile([P, TILES], F32, name="neg_tau")
         gain_col = keep.tile([P, PACK], BF16, name="gain_col")
         scale_col = keep.tile([P, PACK], F32, name="scale_col")
-        v_raw = [keep.tile([P, V_ROWS, D], U8, name="v_raw%d" % h, align_bytes=256) for h in range(V_HALVES)]
+        v_raw = [keep.tile([P, 2, D], U8, name="v_raw%d" % b, align_bytes=256) for b in range(V_PAIRS)]
         k_raw = [keep.tile([P, PACK, D], BF16, name="k_raw%d" % g, align_bytes=256) for g in range(PASSES)]
-        q_raw = keep.tile([P, PASSES, PACK, D], BF16, name="q_raw", align_bytes=256)
+        q_raw = [keep.tile([P, PACK, D], BF16, name="q_raw%d" % g, align_bytes=256) for g in range(PASSES)]
+        q_grouped = [keep.tile([P, PASSES, P, PACK], BF16, name="q_grouped%d" % a, align_bytes=64) for a in range(TILES)]
+        v_bf = [keep.tile([P, 2, D], BF16, name="v_bf%d" % b, align_bytes=64) for b in range(V_PAIRS)]
         k_grouped = [keep.tile([P, D, PACK], BF16, name="k_grouped%d" % g, align_bytes=64) for g in range(PASSES)]
         k_codes = [keep.tile([P, D], U32, name="k_codes%d" % g, align_bytes=64) for g in range(PASSES)]
         k_scales = [keep.tile([P, D], U8, name="k_scales%d" % g, align_bytes=64) for g in range(PASSES)]
         v_codes = [keep.tile([P, 2 * P], U32, name="v_codes%d" % b, align_bytes=64) for b in range(V_PAIRS)]
         v_scales = [keep.tile([P, 2 * P], U8, name="v_scales%d" % b, align_bytes=64) for b in range(V_PAIRS)]
 
-        nc.gpsimd.memset(tau_rows[:], 0.0)
-        make_identity(nc, ident[:])
-        nc.scalar.dma_start(out=scale_col[:], in_=v_scale.rearrange("a b (p t) -> p (a b t)", t=PACK))
-        nc.scalar.dma_start(out=gain_col[:], in_=gain.rearrange("(p t) -> p t", t=PACK))
-        nc.scalar.dma_start(out=tau_rows[0:TILES, :], in_=tau.rearrange("(a p) -> a p", p=P))
         v_rows = v_bytes[0].rearrange("(h p r) j -> h p r j", p=P, r=V_ROWS)
         k_rows = k[0].rearrange("(g p t) c -> g p t c", p=P, t=PACK)
         q_rows = q[0].rearrange("(g p t) c -> g p t c", p=P, t=PACK)
         out_rows = out[0].rearrange("(h p r) i -> h p r i", p=P, r=V_ROWS)
-        nc.sync.dma_start(out=v_raw[0][:], in_=v_rows[0])
-        nc.sync.dma_start(out=k_raw[0][:], in_=k_rows[0])
-        nc.sync.dma_start(out=v_raw[1][:], in_=v_rows[1])
-        nc.sync.dma_start(out=k_raw[1][:], in_=k_rows[1])
-        for g in range(PASSES):
-            nc.sync.dma_start(out=q_raw[:, g], in_=q_rows[g])
-        nc.scalar.activation(out=ident_bf[:], in_=ident[:], func=ACT.Copy)
 
-        scale_bank = psum.tile([P, P, PACK], F32, name="scale_bank", tag="o", bufs=4)
-        for t in range(PACK):
-            nc.tensor.transpose(scale_bank[:, :, t], scale_col[:, t : t + 1].to_broadcast([P, P]), ident[:])
-        tau_bank = psum.tile([P, P], BF16, name="tau_bank", tag="o", bufs=4)
-        nc.tensor.transpose(tau_bank[:], tau_rows[:], ident_bf[:])
+        def bank(number, shape, dtype, name):
+            return psum.tile(shape, dtype, name=name, tag="bank%d" % number)
 
-        def interleave(engine, dst, src):
+        def copy(engine, dst, src):
             if engine is nc.scalar:
                 engine.copy(out=dst, in_=src)
+            elif engine is nc.gpsimd:
+                engine.tensor_scalar(out=dst, in0=src, scalar1=1.0, scalar2=0.0, op0=ALU.mult, op1=ALU.add)
             else:
                 engine.tensor_copy(out=dst, in_=src)
 
+        def v_load(b):
+            h, r0 = divmod(2 * b, V_ROWS)
+            nc.sync.dma_start(out=v_raw[b][:], in_=v_rows[h][:, r0 : r0 + 2, :])
+
+        def k_load(g):
+            nc.sync.dma_start(out=k_raw[g][:], in_=k_rows[g])
+
+        def q_load(g):
+            nc.sync.dma_start(out=q_raw[g][:], in_=q_rows[g])
+
         def k_interleave(engine, g, c0, c1):
-            interleave(
+            copy(
                 engine,
                 k_grouped[g][:, c0:c1, :].rearrange("p (c i) t -> p c t i", i=4),
                 k_raw[g][:, :, c0:c1].rearrange("p t (c i) -> p c t i", i=4),
@@ -89,21 +87,30 @@ def tile_scaledchannelattentioncentredmap_kernel(tc, q, k, v_bytes, v_scale, tau
                 out=k_codes[g][:].bitcast(FP8X4), scales=k_scales[g][:], in_=k_grouped[g][:].rearrange("p c t -> p (c t)")
             )
 
-        v_bf, v_bank, v_grouped = {}, {}, {}
+        v_bank, v_grouped, const = {}, {}, {}
 
-        def v_widen(b):
-            h, r0 = divmod(2 * b, V_ROWS)
-            v_bf[b] = work.tile([P, 2, D], BF16, name="v_bf", align_bytes=64)
-            for r in range(2):
-                nc.vector.tensor_tensor(
-                    out=v_bf[b][:, r, :],
-                    in0=v_raw[h][:, r0 + r, :].bitcast(FP8),
-                    in1=scale_bank[:].rearrange("p m t -> p (m t)"),
-                    op=ALU.mult,
-                )
+        def spread_scale():
+            const["scale"] = bank(7, [P, P, PACK], F32, "scale_bank")
+            for t in range(PACK):
+                nc.tensor.transpose(const["scale"][:, :, t], scale_col[:, t : t + 1].to_broadcast([P, P]), ident[:])
 
-        def v_turn(b):
-            v_bank[b] = psum.tile([P, 2, 2, P], F32, name="v_bank", tag="tr")
+        def tau_turn():
+            const["tau"] = bank(6, [P, P], BF16, "tau_bank")
+            nc.tensor.transpose(const["tau"][:], tau_rows[:], ident_bf[:])
+
+        def tau_scale():
+            nc.scalar.activation(out=neg_tau[:], in_=const["tau"][:, 0:TILES], func=ACT.Copy, scale=-1.0 / 32.0)
+
+        def v_widen(b, r):
+            nc.vector.tensor_tensor(
+                out=v_bf[b][:, r, :],
+                in0=v_raw[b][:, r, :].bitcast(FP8),
+                in1=const["scale"][:].rearrange("p m t -> p (m t)"),
+                op=ALU.mult,
+            )
+
+        def v_turn(b, number):
+            v_bank[b] = bank(number, [P, 2, 2, P], F32, "v_bank")
             for r in range(2):
                 words = v_bf[b][:, r, :].bitcast(F32)
                 for u in range(2):
@@ -120,15 +127,14 @@ def tile_scaledchannelattentioncentredmap_kernel(tc, q, k, v_bytes, v_scale, tau
                 in_=v_grouped[b][:].rearrange("p r n u -> p (r n u)").bitcast(BF16),
             )
 
-        q_grouped, q_codes, q_scales, s_bank, neg_l, neg_max, e, row_sum = {}, {}, {}, {}, {}, {}, {}, {}
+        q_codes, q_scales, s_bank, neg_l, neg_max, e, row_sum = {}, {}, {}, {}, {}, {}, {}
         a_map, a_bank, c_grouped, c_codes, c_scales, o_bank = {}, {}, {}, {}, {}, {}
 
-        def q_interleave(engine, a):
-            q_grouped[a] = work.tile([P, PASSES, P, PACK], BF16, name="q_grouped", align_bytes=64)
-            interleave(
+        def q_interleave(engine, g, a):
+            copy(
                 engine,
-                q_grouped[a][:].rearrange("p g (c i) t -> p g c t i", i=4),
-                q_raw[:, :, :, P * a : P * (a + 1)].rearrange("p g t (c i) -> p g c t i", i=4),
+                q_grouped[a][:, g].rearrange("p (c i) t -> p c t i", i=4),
+                q_raw[g][:, :, P * a : P * (a + 1)].rearrange("p t (c i) -> p c t i", i=4),
             )
 
         def q_quantize(a):
@@ -139,7 +145,7 @@ def tile_scaledchannelattentioncentredmap_kernel(tc, q, k, v_bytes, v_scale, tau
             )
 
         def logits(a):
-            s_bank[a] = psum.tile([P, D], F32, name="s_bank", tag="s")
+            s_bank[a] = bank(a, [P, D], F32, "s_bank")
             for g in range(PASSES):
                 nc.tensor.matmul_mx(
                     out=s_bank[a][:],
@@ -182,20 +188,23 @@ def tile_scaledchannelattentioncentredmap_kernel(tc, q, k, v_bytes, v_scale, tau
             inv_sum[a] = work.tile([P, 1], F32, name="inv_sum")
             nc.vector.reciprocal(out=inv_sum[a][:], in_=row_sum[a][:])
 
-        def normalise(a):
+        def normalise(engine, a):
             a_map[a] = work.tile([P, D], F32, name="a_map")
-            nc.vector.tensor_scalar(out=a_map[a][:], in0=e[a][:], scalar1=inv_sum[a][:], scalar2=None, op0=ALU.mult)
+            if engine is nc.scalar:
+                engine.activation(out=a_map[a][:], in_=e[a][:], func=ACT.Copy, scale=inv_sum[a][:])
+            else:
+                engine.tensor_scalar(out=a_map[a][:], in0=e[a][:], scalar1=inv_sum[a][:], scalar2=None, op0=ALU.mult)
 
         def map_turn(a):
-            a_bank[a] = psum.tile([P, PACK, P], F32, name="a_bank", tag="tr")
+            a_bank[a] = bank(a, [P, P, PACK], F32, "a_bank")
             for t in range(PACK):
-                nc.tensor.transpose(a_bank[a][:, t, :], a_map[a][:, P * t : P * (t + 1)], ident[:])
+                nc.tensor.transpose(a_bank[a][:, :, t], a_map[a][:, P * t : P * (t + 1)], ident[:])
 
         def centre(a):
             c_grouped[a] = work.tile([P, P, PACK], BF16, name="c_grouped", align_bytes=64)
             nc.vector.scalar_tensor_tensor(
                 out=c_grouped[a][:],
-                in0=a_bank[a][:].rearrange("p t i -> p i t"),
+                in0=a_bank[a][:],
                 scalar=1.0 / D,
                 in1=gain_col[:].unsqueeze(1).to_broadcast([P, P, PACK]),
                 op0=ALU.subtract,
@@ -209,97 +218,125 @@ def tile_scaledchannelattentioncentredmap_kernel(tc, q, k, v_bytes, v_scale, tau
                 out=c_codes[a][:].bitcast(FP8X4), scales=c_scales[a][:], in_=c_grouped[a][:].rearrange("p i t -> p (i t)")
             )
 
-        def mix(a):
-            for h in range(V_HALVES):
-                o_bank[a, h] = psum.tile([P, V_ROWS, P], F32, name="o_bank", tag="o", bufs=4)
-                for r in range(V_ROWS):
-                    b, s = divmod(h * V_ROWS + r, 2)
-                    nc.tensor.matmul_mx(
-                        out=o_bank[a, h][:, r, :],
-                        lhsT=v_codes[b][:, P * s : P * (s + 1)].bitcast(FP8X4),
-                        lhsT_scale=v_scales[b][:, P * s : P * (s + 1)],
-                        rhs=c_codes[a][:].bitcast(FP8X4),
-                        rhs_scale=c_scales[a][:],
-                        start=True,
-                        stop=True,
-                    )
+        def mix(a, h, number):
+            o_bank[a, h] = bank(number, [P, V_ROWS, P], F32, "o_bank")
+            for r in range(V_ROWS):
+                b, s = divmod(h * V_ROWS + r, 2)
+                nc.tensor.matmul_mx(
+                    out=o_bank[a, h][:, r, :],
+                    lhsT=v_codes[b][:, P * s : P * (s + 1)].bitcast(FP8X4),
+                    lhsT_scale=v_scales[b][:, P * s : P * (s + 1)],
+                    rhs=c_codes[a][:].bitcast(FP8X4),
+                    rhs_scale=c_scales[a][:],
+                    start=True,
+                    stop=True,
+                )
 
         def store(engine, a, h):
             result = work.tile([P, V_ROWS, P], F32, name="result", align_bytes=256, bufs=8)
-            interleave(engine, result[:], o_bank[a, h][:])
+            copy(engine, result[:], o_bank[a, h][:])
             nc.sync.dma_start(out=out_rows[h][:, :, P * a : P * (a + 1)], in_=result[:])
 
-        v_widen(0)
-        v_turn(0)
-        k_interleave(nc.scalar, 0, 0, D)
-        v_widen(1)
-        v_turn(1)
-        v_widen(2)
-        v_widen(3)
-        nc.scalar.activation(out=neg_tau[:], in_=tau_bank[:, 0:TILES], func=ACT.Copy, scale=-1.0 / 32.0)
+        nc.gpsimd.memset(tau_rows[:], 0.0)
+        make_identity(nc, ident[:])
+        nc.sync.dma_start(out=scale_col[:], in_=v_scale.rearrange("a b (p t) -> p (a b t)", t=PACK))
+        nc.scalar.dma_start(out=gain_col[:], in_=gain.rearrange("(p t) -> p t", t=PACK))
+        nc.scalar.dma_start(out=tau_rows[0:TILES, :], in_=tau.rearrange("(a p) -> a p", p=P))
+        v_load(0)
+        k_load(0)
+        v_load(1)
+        k_load(1)
+        q_load(0)
+        q_load(1)
+        v_load(2)
+        v_load(3)
+        nc.scalar.activation(out=ident_bf[:], in_=ident[:], func=ACT.Copy)
+        spread_scale()
+        v_widen(0, 0)
+        v_widen(0, 1)
+        k_interleave(nc.scalar, 0, 0, 256)
+        k_interleave(nc.vector, 0, 256, 512)
+        v_turn(0, 4)
+        v_widen(1, 0)
+        v_widen(1, 1)
+        v_turn(1, 5)
         v_copy_out(0)
-        v_turn(2)
-        v_copy_out(1)
-        v_turn(3)
+        k_interleave(nc.scalar, 1, 0, 320)
         k_quantize(0)
-        k_interleave(nc.scalar, 1, 0, K1_SCALAR_COLS)
-        k_interleave(nc.vector, 1, K1_SCALAR_COLS, D)
-        q_interleave(nc.vector, 0)
-        v_quantize(0)
-        q_quantize(0)
+        k_interleave(nc.vector, 1, 320, 512)
+        q_interleave(nc.scalar, 0, 0)
+        q_interleave(nc.scalar, 0, 1)
         k_quantize(1)
+        q_interleave(nc.vector, 1, 0)
+        q_interleave(nc.vector, 1, 1)
+        tau_turn()
+        q_quantize(0)
         logits(0)
-        q_interleave(nc.scalar, 1)
-        v_quantize(1)
+        v_copy_out(1)
+        q_interleave(nc.scalar, 0, 2)
+        q_interleave(nc.scalar, 1, 2)
         q_quantize(1)
         logits(1)
+        tau_scale()
+        v_widen(2, 0)
+        v_widen(2, 1)
+        v_turn(2, 4)
+        q_interleave(nc.scalar, 0, 3)
+        q_interleave(nc.scalar, 1, 3)
         row_max(0)
-        q_interleave(nc.scalar, 2)
         exponentials(0)
         q_quantize(2)
         logits(2)
         row_max(1)
-        v_copy_out(2)
-        v_copy_out(3)
         exponentials(1)
-        q_interleave(nc.scalar, 3)
-        invert(0)
-        v_quantize(2)
-        normalise(0)
-        map_turn(0)
-        v_quantize(3)
-        invert(1)
-        row_max(2)
-        exponentials(2)
         q_quantize(3)
         logits(3)
-        normalise(1)
+        invert(0)
+        normalise(nc.scalar, 0)
+        map_turn(0)
+        row_max(2)
+        exponentials(2)
+        invert(1)
+        normalise(nc.scalar, 1)
         map_turn(1)
-        centre(0)
-        invert(2)
-        c_quantize(0)
-        mix(0)
+        v_quantize(0)
         row_max(3)
         exponentials(3)
-        normalise(2)
-        map_turn(2)
-        centre(1)
+        invert(2)
+        v_quantize(1)
+        normalise(nc.scalar, 2)
+        centre(0)
+        v_copy_out(2)
+        v_widen(3, 0)
         invert(3)
-        c_quantize(1)
-        store(nc.scalar, 0, 0)
-        store(nc.scalar, 0, 1)
-        mix(1)
-        normalise(3)
+        c_quantize(0)
+        normalise(nc.scalar, 3)
+        map_turn(2)
+        mix(0, 0, 6)
+        centre(1)
+        v_widen(3, 1)
         map_turn(3)
+        c_quantize(1)
+        v_turn(3, 5)
+        mix(1, 0, 4)
+        store(nc.scalar, 0, 0)
+        v_quantize(2)
         centre(2)
+        v_copy_out(3)
         store(nc.scalar, 1, 0)
-        store(nc.scalar, 1, 1)
-        c_quantize(2)
-        mix(2)
         centre(3)
-        store(nc.scalar, 2, 0)
-        store(nc.scalar, 2, 1)
+        c_quantize(2)
+        mix(2, 0, 7)
+        v_quantize(3)
+        mix(0, 1, 6)
         c_quantize(3)
-        mix(3)
-        store(nc.scalar, 3, 0)
+        mix(1, 1, 5)
+        mix(3, 0, 0)
+        mix(2, 1, 4)
+        mix(3, 1, 1)
+        store(nc.scalar, 2, 0)
+        store(nc.vector, 0, 1)
+        store(nc.scalar, 1, 1)
+        store(nc.vector, 3, 0)
+        store(nc.scalar, 2, 1)
         store(nc.vector, 3, 1)

@@ -41,7 +41,10 @@ def tile_scaledchannelattentioncentredmap_kernel(tc, q, k, v_bytes, v_scale, tau
         v_raw = [keep.tile([P, 2, D], U8, name="v_raw%d" % b, align_bytes=256) for b in range(V_PAIRS)]
         k_raw = [keep.tile([P, PACK, D], BF16, name="k_raw%d" % g, align_bytes=256) for g in range(PASSES)]
         q_raw = [keep.tile([P, PACK, D], BF16, name="q_raw%d" % g, align_bytes=256) for g in range(PASSES)]
-        q_grouped = [keep.tile([P, PASSES, P, PACK], BF16, name="q_grouped%d" % a, align_bytes=64) for a in range(TILES)]
+        q_parts = [[(0, D)], [(P * a, P * (a + 1)) for a in range(TILES)]]
+        q_grouped = [[keep.tile([P, c1 - c0, PACK], BF16, name="q_grouped%d_%d" % (g, c0), align_bytes=64) for c0, c1 in q_parts[g]] for g in range(PASSES)]
+        q_codes = [[keep.tile([P, c1 - c0], U32, name="q_codes%d_%d" % (g, c0), align_bytes=64) for c0, c1 in q_parts[g]] for g in range(PASSES)]
+        q_scales = [[keep.tile([P, c1 - c0], U8, name="q_scales%d_%d" % (g, c0), align_bytes=64) for c0, c1 in q_parts[g]] for g in range(PASSES)]
         v_bf = [keep.tile([P, 2, D], BF16, name="v_bf%d" % b, align_bytes=64) for b in range(V_PAIRS)]
         k_grouped = [keep.tile([P, D, PACK], BF16, name="k_grouped%d" % g, align_bytes=64) for g in range(PASSES)]
         k_codes = [keep.tile([P, D], U32, name="k_codes%d" % g, align_bytes=64) for g in range(PASSES)]
@@ -75,12 +78,14 @@ def tile_scaledchannelattentioncentredmap_kernel(tc, q, k, v_bytes, v_scale, tau
         def q_load(g):
             nc.sync.dma_start(out=q_raw[g][:], in_=q_rows[g])
 
+        def interleave(engine, grouped, raw):
+            if engine is nc.gpsimd:
+                copy(engine, grouped, raw.rearrange("p t c -> p c t"))
+            else:
+                copy(engine, grouped.rearrange("p (c i) t -> p c t i", i=4), raw.rearrange("p t (c i) -> p c t i", i=4))
+
         def k_interleave(engine, g, c0, c1):
-            copy(
-                engine,
-                k_grouped[g][:, c0:c1, :].rearrange("p (c i) t -> p c t i", i=4),
-                k_raw[g][:, :, c0:c1].rearrange("p t (c i) -> p c t i", i=4),
-            )
+            interleave(engine, k_grouped[g][:, c0:c1, :], k_raw[g][:, :, c0:c1])
 
         def k_quantize(g):
             nc.vector.quantize_mx(
@@ -127,35 +132,35 @@ def tile_scaledchannelattentioncentredmap_kernel(tc, q, k, v_bytes, v_scale, tau
                 in_=v_grouped[b][:].rearrange("p r n u -> p (r n u)").bitcast(BF16),
             )
 
-        q_codes, q_scales, s_bank, neg_l, neg_max, e, row_sum = {}, {}, {}, {}, {}, {}, {}
+        s_bank, neg_l, neg_max, e, row_sum = {}, {}, {}, {}, {}
         a_map, a_bank, c_grouped, c_codes, c_scales, o_bank = {}, {}, {}, {}, {}, {}
 
-        def q_interleave(engine, g, a):
-            copy(
-                engine,
-                q_grouped[a][:, g].rearrange("p (c i) t -> p c t i", i=4),
-                q_raw[g][:, :, P * a : P * (a + 1)].rearrange("p t (c i) -> p c t i", i=4),
-            )
+        def q_interleave(engine, g, part, c0, c1):
+            base = q_parts[g][part][0]
+            interleave(engine, q_grouped[g][part][:, c0 - base : c1 - base, :], q_raw[g][:, :, c0:c1])
 
-        def q_quantize(a):
-            q_codes[a] = work.tile([P, PASSES * P], U32, name="q_codes", align_bytes=64)
-            q_scales[a] = work.tile([P, PASSES * P], U8, name="q_scales", align_bytes=64)
+        def q_quantize(g, part):
             nc.vector.quantize_mx(
-                out=q_codes[a][:].bitcast(FP8X4), scales=q_scales[a][:], in_=q_grouped[a][:].rearrange("p g c t -> p (g c t)")
+                out=q_codes[g][part][:].bitcast(FP8X4),
+                scales=q_scales[g][part][:],
+                in_=q_grouped[g][part][:].rearrange("p c t -> p (c t)"),
             )
 
-        def logits(a):
-            s_bank[a] = bank(a, [P, D], F32, "s_bank")
-            for g in range(PASSES):
-                nc.tensor.matmul_mx(
-                    out=s_bank[a][:],
-                    lhsT=q_codes[a][:, P * g : P * (g + 1)].bitcast(FP8X4),
-                    lhsT_scale=q_scales[a][:, P * g : P * (g + 1)],
-                    rhs=k_codes[g][:].bitcast(FP8X4),
-                    rhs_scale=k_scales[g][:],
-                    start=(g == 0),
-                    stop=(g == PASSES - 1),
-                )
+        def logits(a, g):
+            if g == 0:
+                s_bank[a] = bank(a, [P, D], F32, "s_bank")
+                part, cols = 0, slice(P * a, P * (a + 1))
+            else:
+                part, cols = a, slice(0, P)
+            nc.tensor.matmul_mx(
+                out=s_bank[a][:],
+                lhsT=q_codes[g][part][:, cols].bitcast(FP8X4),
+                lhsT_scale=q_scales[g][part][:, cols],
+                rhs=k_codes[g][:].bitcast(FP8X4),
+                rhs_scale=k_scales[g][:],
+                start=(g == 0),
+                stop=(g == PASSES - 1),
+            )
 
         def row_max(a):
             neg_l[a] = work.tile([P, PACK, P], F32, name="neg_l")
@@ -245,98 +250,101 @@ def tile_scaledchannelattentioncentredmap_kernel(tc, q, k, v_bytes, v_scale, tau
         v_load(0)
         k_load(0)
         v_load(1)
-        k_load(1)
         q_load(0)
-        q_load(1)
         v_load(2)
         v_load(3)
+        k_load(1)
+        q_load(1)
         nc.scalar.activation(out=ident_bf[:], in_=ident[:], func=ACT.Copy)
         spread_scale()
         v_widen(0, 0)
         v_widen(0, 1)
         k_interleave(nc.scalar, 0, 0, 256)
-        k_interleave(nc.vector, 0, 256, 512)
+        k_interleave(nc.gpsimd, 0, 256, 512)
+        tau_turn()
+        tau_scale()
         v_turn(0, 4)
         v_widen(1, 0)
         v_widen(1, 1)
         v_turn(1, 5)
-        v_copy_out(0)
-        k_interleave(nc.scalar, 1, 0, 320)
-        k_quantize(0)
-        k_interleave(nc.vector, 1, 320, 512)
-        q_interleave(nc.scalar, 0, 0)
-        q_interleave(nc.scalar, 0, 1)
-        k_quantize(1)
-        q_interleave(nc.vector, 1, 0)
-        q_interleave(nc.vector, 1, 1)
-        tau_turn()
-        q_quantize(0)
-        logits(0)
-        v_copy_out(1)
-        q_interleave(nc.scalar, 0, 2)
-        q_interleave(nc.scalar, 1, 2)
-        q_quantize(1)
-        logits(1)
-        tau_scale()
+        q_interleave(nc.scalar, 0, 0, 0, 192)
+        q_interleave(nc.gpsimd, 0, 0, 192, 512)
         v_widen(2, 0)
         v_widen(2, 1)
-        v_turn(2, 4)
-        q_interleave(nc.scalar, 0, 3)
-        q_interleave(nc.scalar, 1, 3)
+        v_turn(2, 6)
+        v_copy_out(0)
+        v_widen(3, 0)
+        v_widen(3, 1)
+        v_turn(3, 4)
+        k_interleave(nc.scalar, 1, 0, 320)
+        k_quantize(0)
+        q_quantize(0, 0)
+        logits(0, 0)
+        logits(1, 0)
+        logits(2, 0)
+        k_interleave(nc.vector, 1, 320, 512)
+        q_interleave(nc.scalar, 1, 0, 0, 128)
+        q_interleave(nc.scalar, 1, 1, 128, 256)
+        q_quantize(1, 0)
+        k_quantize(1)
+        logits(0, 1)
+        q_interleave(nc.scalar, 1, 2, 256, 384)
+        q_quantize(1, 1)
+        logits(1, 1)
+        logits(3, 0)
+        v_copy_out(1)
+        q_quantize(1, 2)
+        logits(2, 1)
+        q_interleave(nc.scalar, 1, 3, 384, 512)
+        v_quantize(0)
         row_max(0)
         exponentials(0)
-        q_quantize(2)
-        logits(2)
         row_max(1)
         exponentials(1)
-        q_quantize(3)
-        logits(3)
-        invert(0)
-        normalise(nc.scalar, 0)
-        map_turn(0)
         row_max(2)
         exponentials(2)
+        invert(0)
+        q_quantize(1, 3)
+        logits(3, 1)
         invert(1)
-        normalise(nc.scalar, 1)
+        normalise(nc.vector, 0)
+        map_turn(0)
+        v_copy_out(2)
+        normalise(nc.vector, 1)
         map_turn(1)
-        v_quantize(0)
+        invert(2)
+        normalise(nc.scalar, 2)
+        map_turn(2)
+        v_copy_out(3)
         row_max(3)
         exponentials(3)
-        invert(2)
         v_quantize(1)
-        normalise(nc.scalar, 2)
         centre(0)
-        v_copy_out(2)
-        v_widen(3, 0)
-        invert(3)
-        c_quantize(0)
-        normalise(nc.scalar, 3)
-        map_turn(2)
-        mix(0, 0, 6)
-        centre(1)
-        v_widen(3, 1)
-        map_turn(3)
-        c_quantize(1)
-        v_turn(3, 5)
-        mix(1, 0, 4)
-        store(nc.scalar, 0, 0)
         v_quantize(2)
-        centre(2)
-        v_copy_out(3)
-        store(nc.scalar, 1, 0)
-        centre(3)
-        c_quantize(2)
-        mix(2, 0, 7)
+        c_quantize(0)
+        invert(3)
+        normalise(nc.scalar, 3)
         v_quantize(3)
-        mix(0, 1, 6)
-        c_quantize(3)
+        mix(0, 0, 6)
+        mix(0, 1, 7)
+        map_turn(3)
+        centre(1)
+        store(nc.scalar, 0, 0)
+        store(nc.scalar, 0, 1)
+        c_quantize(1)
+        mix(1, 0, 4)
         mix(1, 1, 5)
-        mix(3, 0, 0)
-        mix(2, 1, 4)
-        mix(3, 1, 1)
-        store(nc.scalar, 2, 0)
-        store(nc.vector, 0, 1)
+        centre(2)
+        c_quantize(2)
+        mix(2, 0, 0)
+        mix(2, 1, 1)
+        centre(3)
+        store(nc.scalar, 1, 0)
         store(nc.scalar, 1, 1)
-        store(nc.vector, 3, 0)
+        c_quantize(3)
+        mix(3, 0, 6)
+        mix(3, 1, 7)
+        store(nc.vector, 2, 0)
         store(nc.scalar, 2, 1)
-        store(nc.vector, 3, 1)
+        store(nc.vector, 3, 0)
+        store(nc.scalar, 3, 1)

@@ -252,51 +252,50 @@ def tile_scaledchannelattentioncentredmap_kernel(tc, q, k, v_bytes, v_scale, tau
         v_load(1)
         q_load(0)
         v_load(2)
-        v_load(3)
         k_load(1)
+        v_load(3)
         q_load(1)
         nc.scalar.activation(out=ident_bf[:], in_=ident[:], func=ACT.Copy)
         spread_scale()
         v_widen(0, 0)
         v_widen(0, 1)
-        k_interleave(nc.scalar, 0, 0, 256)
-        k_interleave(nc.gpsimd, 0, 256, 512)
+        k_interleave(nc.scalar, 0, 0, 320)
+        k_interleave(nc.vector, 0, 320, 512)
         tau_turn()
         tau_scale()
         v_turn(0, 4)
         v_widen(1, 0)
         v_widen(1, 1)
         v_turn(1, 5)
-        q_interleave(nc.scalar, 0, 0, 0, 192)
-        q_interleave(nc.gpsimd, 0, 0, 192, 512)
+        q_interleave(nc.scalar, 0, 0, 0, 320)
+        v_copy_out(0)
         v_widen(2, 0)
         v_widen(2, 1)
         v_turn(2, 6)
-        v_copy_out(0)
-        v_widen(3, 0)
-        v_widen(3, 1)
-        v_turn(3, 4)
-        k_interleave(nc.scalar, 1, 0, 320)
+        q_interleave(nc.vector, 0, 0, 320, 512)
         k_quantize(0)
         q_quantize(0, 0)
         logits(0, 0)
         logits(1, 0)
         logits(2, 0)
+        logits(3, 0)
+        k_interleave(nc.scalar, 1, 0, 320)
         k_interleave(nc.vector, 1, 320, 512)
+        v_widen(3, 0)
         q_interleave(nc.scalar, 1, 0, 0, 128)
         q_interleave(nc.scalar, 1, 1, 128, 256)
-        q_quantize(1, 0)
         k_quantize(1)
-        logits(0, 1)
         q_interleave(nc.scalar, 1, 2, 256, 384)
+        q_quantize(1, 0)
+        logits(0, 1)
         q_quantize(1, 1)
         logits(1, 1)
-        logits(3, 0)
         v_copy_out(1)
+        v_widen(3, 1)
         q_quantize(1, 2)
         logits(2, 1)
+        v_turn(3, 4)
         q_interleave(nc.scalar, 1, 3, 384, 512)
-        v_quantize(0)
         row_max(0)
         exponentials(0)
         row_max(1)
@@ -309,31 +308,32 @@ def tile_scaledchannelattentioncentredmap_kernel(tc, q, k, v_bytes, v_scale, tau
         invert(1)
         normalise(nc.vector, 0)
         map_turn(0)
-        v_copy_out(2)
         normalise(nc.vector, 1)
         map_turn(1)
+        v_copy_out(2)
         invert(2)
         normalise(nc.scalar, 2)
         map_turn(2)
-        v_copy_out(3)
         row_max(3)
         exponentials(3)
-        v_quantize(1)
+        v_copy_out(3)
+        v_quantize(0)
         centre(0)
-        v_quantize(2)
+        v_quantize(1)
         c_quantize(0)
+        mix(0, 0, 5)
         invert(3)
         normalise(nc.scalar, 3)
+        v_quantize(2)
         v_quantize(3)
-        mix(0, 0, 6)
-        mix(0, 1, 7)
+        mix(0, 1, 6)
         map_turn(3)
         centre(1)
         store(nc.scalar, 0, 0)
         store(nc.scalar, 0, 1)
         c_quantize(1)
-        mix(1, 0, 4)
-        mix(1, 1, 5)
+        mix(1, 0, 7)
+        mix(1, 1, 4)
         centre(2)
         c_quantize(2)
         mix(2, 0, 0)
@@ -342,8 +342,8 @@ def tile_scaledchannelattentioncentredmap_kernel(tc, q, k, v_bytes, v_scale, tau
         store(nc.scalar, 1, 0)
         store(nc.scalar, 1, 1)
         c_quantize(3)
-        mix(3, 0, 6)
-        mix(3, 1, 7)
+        mix(3, 0, 5)
+        mix(3, 1, 6)
         store(nc.vector, 2, 0)
         store(nc.scalar, 2, 1)
         store(nc.vector, 3, 0)

from contextlib import ExitStack

import concourse.mybir as mybir
from concourse.masks import make_identity

N, D = 1024, 512
FLOPS = 2 * 2 * N * D * D

F32 = mybir.dt.float32
BF16 = mybir.dt.bfloat16
U32 = mybir.dt.uint32
U8 = mybir.dt.uint8
FP8 = mybir.dt.float8_e4m3fn
FP8X4 = mybir.dt.float8_e4m3fn_x4
ALU = mybir.AluOpType
ACT = mybir.ActivationFunctionType

P = 128
PACK = 4
PASSES = N // (P * PACK)
TILES = D // P
V_HALVES = 2
V_ROWS = N // (V_HALVES * P)
V_PAIRS = N // (2 * P)


def tile_scaledchannelattentioncentredmap_kernel(tc, q, k, v_bytes, v_scale, tau, gain, out):
    nc = tc.nc
    with ExitStack() as ctx:
        keep = ctx.enter_context(tc.tile_pool(name="keep", bufs=1))
        work = ctx.enter_context(tc.tile_pool(name="work", bufs=4))
        psum = ctx.enter_context(tc.psum_pool(name="psum", bufs=1))
        ctx.enter_context(tc.manual_schedule())

        ident = keep.tile([P, P], F32, name="ident")
        ident_bf = keep.tile([P, P], BF16, name="ident_bf")
        tau_rows = keep.tile([P, P], BF16, name="tau_rows")
        neg_tau = keep.tile([P, TILES], F32, name="neg_tau")
        gain_col = keep.tile([P, PACK], BF16, name="gain_col")
        scale_col = keep.tile([P, PACK], F32, name="scale_col")
        v_raw = [keep.tile([P, 2, D], U8, name="v_raw%d" % b, align_bytes=256) for b in range(V_PAIRS)]
        k_raw = [keep.tile([P, PACK, D], BF16, name="k_raw%d" % g, align_bytes=256) for g in range(PASSES)]
        q_raw = [keep.tile([P, PACK, D], BF16, name="q_raw%d" % g, align_bytes=256) for g in range(PASSES)]
        q_parts = [[(0, D)], [(P * a, P * (a + 1)) for a in range(TILES)]]
        q_grouped = [[keep.tile([P, c1 - c0, PACK], BF16, name="q_grouped%d_%d" % (g, c0), align_bytes=64) for c0, c1 in q_parts[g]] for g in range(PASSES)]
        q_codes = [[keep.tile([P, c1 - c0], U32, name="q_codes%d_%d" % (g, c0), align_bytes=64) for c0, c1 in q_parts[g]] for g in range(PASSES)]
        q_scales = [[keep.tile([P, c1 - c0], U8, name="q_scales%d_%d" % (g, c0), align_bytes=64) for c0, c1 in q_parts[g]] for g in range(PASSES)]
        v_bf = [keep.tile([P, 2, D], BF16, name="v_bf%d" % b, align_bytes=64) for b in range(V_PAIRS)]
        k_grouped = [keep.tile([P, D, PACK], BF16, name="k_grouped%d" % g, align_bytes=64) for g in range(PASSES)]
        k_codes = [keep.tile([P, D], U32, name="k_codes%d" % g, align_bytes=64) for g in range(PASSES)]
        k_scales = [keep.tile([P, D], U8, name="k_scales%d" % g, align_bytes=64) for g in range(PASSES)]
        v_codes = [keep.tile([P, 2 * P], U32, name="v_codes%d" % b, align_bytes=64) for b in range(V_PAIRS)]
        v_scales = [keep.tile([P, 2 * P], U8, name="v_scales%d" % b, align_bytes=64) for b in range(V_PAIRS)]

        v_rows = v_bytes[0].rearrange("(h p r) j -> h p r j", p=P, r=V_ROWS)
        k_rows = k[0].rearrange("(g p t) c -> g p t c", p=P, t=PACK)
        q_rows = q[0].rearrange("(g p t) c -> g p t c", p=P, t=PACK)
        out_rows = out[0].rearrange("(h p r) i -> h p r i", p=P, r=V_ROWS)

        def bank(number, shape, dtype, name):
            return psum.tile(shape, dtype, name=name, tag="bank%d" % number)

        def copy(engine, dst, src):
            if engine is nc.scalar:
                engine.copy(out=dst, in_=src)
            elif engine is nc.gpsimd:
                engine.tensor_scalar(out=dst, in0=src, scalar1=1.0, scalar2=0.0, op0=ALU.mult, op1=ALU.add)
            else:
                engine.tensor_copy(out=dst, in_=src)

        def v_load(b):
            h, r0 = divmod(2 * b, V_ROWS)
            nc.sync.dma_start(out=v_raw[b][:], in_=v_rows[h][:, r0 : r0 + 2, :])

        def k_load(g):
            nc.sync.dma_start(out=k_raw[g][:], in_=k_rows[g])

        def q_load(g):
            nc.sync.dma_start(out=q_raw[g][:], in_=q_rows[g])

        def interleave(engine, grouped, raw):
            if engine is nc.gpsimd:
                copy(engine, grouped, raw.rearrange("p t c -> p c t"))
            else:
                copy(engine, grouped.rearrange("p (c i) t -> p c t i", i=4), raw.rearrange("p t (c i) -> p c t i", i=4))

        def k_interleave(engine, g, c0, c1):
            interleave(engine, k_grouped[g][:, c0:c1, :], k_raw[g][:, :, c0:c1])

        def k_quantize(g):
            nc.vector.quantize_mx(
                out=k_codes[g][:].bitcast(FP8X4), scales=k_scales[g][:], in_=k_grouped[g][:].rearrange("p c t -> p (c t)")
            )

        v_bank, v_grouped, const = {}, {}, {}

        def spread_scale():
            const["scale"] = bank(7, [P, P, PACK], F32, "scale_bank")
            for t in range(PACK):
                nc.tensor.transpose(const["scale"][:, :, t], scale_col[:, t : t + 1].to_broadcast([P, P]), ident[:])

        def tau_turn():
            const["tau"] = bank(6, [P, P], BF16, "tau_bank")
            nc.tensor.transpose(const["tau"][:], tau_rows[:], ident_bf[:])

        def tau_scale():
            nc.scalar.activation(out=neg_tau[:], in_=const["tau"][:, 0:TILES], func=ACT.Copy, scale=-1.0 / 32.0)

        def v_widen(b, r):
            nc.vector.tensor_tensor(
                out=v_bf[b][:, r, :],
                in0=v_raw[b][:, r, :].bitcast(FP8),
                in1=const["scale"][:].rearrange("p m t -> p (m t)"),
                op=ALU.mult,
            )

        def v_turn(b, number):
            v_bank[b] = bank(number, [P, 2, 2, P], F32, "v_bank")
            for r in range(2):
                words = v_bf[b][:, r, :].bitcast(F32)
                for u in range(2):
                    nc.tensor.transpose(v_bank[b][:, r, u, :], words[:, u : 2 * P : 2], ident[:])

        def v_copy_out(b):
            v_grouped[b] = work.tile([P, 2, P, 2], F32, name="v_grouped", align_bytes=64)
            nc.scalar.copy(out=v_grouped[b][:], in_=v_bank[b][:].rearrange("p r u n -> p r n u"))

        def v_quantize(b):
            nc.vector.quantize_mx(
                out=v_codes[b][:].bitcast(FP8X4),
                scales=v_scales[b][:],
                in_=v_grouped[b][:].rearrange("p r n u -> p (r n u)").bitcast(BF16),
            )

        s_bank, neg_l, neg_max, e, row_sum = {}, {}, {}, {}, {}
        a_map, a_bank, c_grouped, c_codes, c_scales, o_bank = {}, {}, {}, {}, {}, {}

        def q_interleave(engine, g, part, c0, c1):
            base = q_parts[g][part][0]
            interleave(engine, q_grouped[g][part][:, c0 - base : c1 - base, :], q_raw[g][:, :, c0:c1])

        def q_quantize(g, part):
            nc.vector.quantize_mx(
                out=q_codes[g][part][:].bitcast(FP8X4),
                scales=q_scales[g][part][:],
                in_=q_grouped[g][part][:].rearrange("p c t -> p (c t)"),
            )

        def logits(a, g):
            if g == 0:
                s_bank[a] = bank(a, [P, D], F32, "s_bank")
                part, cols = 0, slice(P * a, P * (a + 1))
            else:
                part, cols = a, slice(0, P)
            nc.tensor.matmul_mx(
                out=s_bank[a][:],
                lhsT=q_codes[g][part][:, cols].bitcast(FP8X4),
                lhsT_scale=q_scales[g][part][:, cols],
                rhs=k_codes[g][:].bitcast(FP8X4),
                rhs_scale=k_scales[g][:],
                start=(g == 0),
                stop=(g == PASSES - 1),
            )

        def row_max(a):
            neg_l[a] = work.tile([P, PACK, P], F32, name="neg_l")
            neg_max[a] = work.tile([P, 1], F32, name="neg_max")
            nc.vector.tensor_scalar(
                out=neg_l[a][:],
                in0=s_bank[a][:].rearrange("p (m t) -> p t m", t=PACK),
                scalar1=neg_tau[:, a : a + 1],
                scalar2=None,
                op0=ALU.mult,
                op1=ALU.min,
                accum_out=neg_max[a][:],
            )

        def exponentials(a):
            e[a] = work.tile([P, D], F32, name="e")
            row_sum[a] = work.tile([P, 1], F32, name="row_sum")
            nc.scalar.activation(
                out=e[a][:],
                in_=neg_l[a][:].rearrange("p t m -> p (t m)"),
                func=ACT.Exp,
                scale=-1.0,
                bias=neg_max[a][:],
                accum_out=row_sum[a][:],
            )

        inv_sum = {}

        def invert(a):
            inv_sum[a] = work.tile([P, 1], F32, name="inv_sum")
            nc.vector.reciprocal(out=inv_sum[a][:], in_=row_sum[a][:])

        def normalise(engine, a):
            a_map[a] = work.tile([P, D], F32, name="a_map")
            if engine is nc.scalar:
                engine.activation(out=a_map[a][:], in_=e[a][:], func=ACT.Copy, scale=inv_sum[a][:])
            else:
                engine.tensor_scalar(out=a_map[a][:], in0=e[a][:], scalar1=inv_sum[a][:], scalar2=None, op0=ALU.mult)

        def map_turn(a):
            a_bank[a] = bank(a, [P, P, PACK], F32, "a_bank")
            for t in range(PACK):
                nc.tensor.transpose(a_bank[a][:, :, t], a_map[a][:, P * t : P * (t + 1)], ident[:])

        def centre(a):
            c_grouped[a] = work.tile([P, P, PACK], BF16, name="c_grouped", align_bytes=64)
            nc.vector.scalar_tensor_tensor(
                out=c_grouped[a][:],
                in0=a_bank[a][:],
                scalar=1.0 / D,
                in1=gain_col[:].unsqueeze(1).to_broadcast([P, P, PACK]),
                op0=ALU.subtract,
                op1=ALU.mult,
            )

        def c_quantize(a):
            c_codes[a] = work.tile([P, P], U32, name="c_codes", align_bytes=64)
            c_scales[a] = work.tile([P, P], U8, name="c_scales", align_bytes=64)
            nc.vector.quantize_mx(
                out=c_codes[a][:].bitcast(FP8X4), scales=c_scales[a][:], in_=c_grouped[a][:].rearrange("p i t -> p (i t)")
            )

        def mix(a, h, number):
            o_bank[a, h] = bank(number, [P, V_ROWS, P], F32, "o_bank")
            for r in range(V_ROWS):
                b, s = divmod(h * V_ROWS + r, 2)
                nc.tensor.matmul_mx(
                    out=o_bank[a, h][:, r, :],
                    lhsT=v_codes[b][:, P * s : P * (s + 1)].bitcast(FP8X4),
                    lhsT_scale=v_scales[b][:, P * s : P * (s + 1)],
                    rhs=c_codes[a][:].bitcast(FP8X4),
                    rhs_scale=c_scales[a][:],
                    start=True,
                    stop=True,
                )

        def store(engine, a, h):
            result = work.tile([P, V_ROWS, P], F32, name="result", align_bytes=256, bufs=8)
            copy(engine, result[:], o_bank[a, h][:])
            nc.sync.dma_start(out=out_rows[h][:, :, P * a : P * (a + 1)], in_=result[:])

        nc.gpsimd.memset(tau_rows[:], 0.0)
        make_identity(nc, ident[:])
        nc.sync.dma_start(out=scale_col[:], in_=v_scale.rearrange("a b (p t) -> p (a b t)", t=PACK))
        nc.scalar.dma_start(out=gain_col[:], in_=gain.rearrange("(p t) -> p t", t=PACK))
        nc.scalar.dma_start(out=tau_rows[0:TILES, :], in_=tau.rearrange("(a p) -> a p", p=P))
        v_load(0)
        k_load(0)
        v_load(1)
        q_load(0)
        v_load(2)
        k_load(1)
        v_load(3)
        q_load(1)
        nc.scalar.activation(out=ident_bf[:], in_=ident[:], func=ACT.Copy)
        spread_scale()
        v_widen(0, 0)
        v_widen(0, 1)
        k_interleave(nc.scalar, 0, 0, 320)
        k_interleave(nc.vector, 0, 320, 512)
        tau_turn()
        tau_scale()
        v_turn(0, 4)
        v_widen(1, 0)
        v_widen(1, 1)
        v_turn(1, 5)
        q_interleave(nc.scalar, 0, 0, 0, 320)
        v_copy_out(0)
        v_widen(2, 0)
        v_widen(2, 1)
        v_turn(2, 6)
        q_interleave(nc.vector, 0, 0, 320, 512)
        k_quantize(0)
        q_quantize(0, 0)
        logits(0, 0)
        logits(1, 0)
        logits(2, 0)
        logits(3, 0)
        k_interleave(nc.scalar, 1, 0, 320)
        k_interleave(nc.vector, 1, 320, 512)
        v_widen(3, 0)
        q_interleave(nc.scalar, 1, 0, 0, 128)
        q_interleave(nc.scalar, 1, 1, 128, 256)
        k_quantize(1)
        q_interleave(nc.scalar, 1, 2, 256, 384)
        q_quantize(1, 0)
        logits(0, 1)
        q_quantize(1, 1)
        logits(1, 1)
        v_copy_out(1)
        v_widen(3, 1)
        q_quantize(1, 2)
        logits(2, 1)
        v_turn(3, 4)
        q_interleave(nc.scalar, 1, 3, 384, 512)
        row_max(0)
        exponentials(0)
        row_max(1)
        exponentials(1)
        row_max(2)
        exponentials(2)
        invert(0)
        q_quantize(1, 3)
        logits(3, 1)
        invert(1)
        normalise(nc.vector, 0)
        map_turn(0)
        normalise(nc.vector, 1)
        map_turn(1)
        v_copy_out(2)
        invert(2)
        normalise(nc.scalar, 2)
        map_turn(2)
        row_max(3)
        exponentials(3)
        v_copy_out(3)
        v_quantize(0)
        centre(0)
        v_quantize(1)
        c_quantize(0)
        mix(0, 0, 5)
        invert(3)
        normalise(nc.scalar, 3)
        v_quantize(2)
        v_quantize(3)
        mix(0, 1, 6)
        map_turn(3)
        centre(1)
        store(nc.scalar, 0, 0)
        store(nc.scalar, 0, 1)
        c_quantize(1)
        mix(1, 0, 7)
        mix(1, 1, 4)
        centre(2)
        c_quantize(2)
        mix(2, 0, 0)
        mix(2, 1, 1)
        centre(3)
        store(nc.scalar, 1, 0)
        store(nc.scalar, 1, 1)
        c_quantize(3)
        mix(3, 0, 5)
        mix(3, 1, 6)
        store(nc.vector, 2, 0)
        store(nc.scalar, 2, 1)
        store(nc.vector, 3, 0)
        store(nc.scalar, 3, 1)
